import numpy as np
import ml_dtypes


def mxq(x, axis, fmt="e4m3"):
    dtype, down = {"e4m3": (ml_dtypes.float8_e4m3fn, 7), "e5m2": (ml_dtypes.float8_e5m2, 14)}[fmt]
    v = np.moveaxis(np.asarray(x, np.float32).astype(ml_dtypes.bfloat16).astype(np.float64), axis, -1)
    blocks = v.reshape(v.shape[:-1] + (-1, 32))
    amax = np.abs(blocks).max(-1, keepdims=True)
    byte = np.maximum(np.where(amax > 0, np.frexp(amax)[1] - 1 + 127, 0) - down, 1)
    scale = np.exp2(byte - 127.0)
    codes = (blocks / scale).astype(np.float32).astype(dtype).astype(np.float64)
    return np.moveaxis((codes * scale).reshape(v.shape), -1, axis)


WIDE = False


def mx_kscale(k):
    if not WIDE:
        return np.ones(k)
    levels = np.array([10, -10, 5, -5, 0])
    if k % 512:
        return np.exp2(np.random.permutation(np.resize(levels, k // 32))).repeat(32)
    a = np.empty((k // 512, 16))
    for p in range(k // 512):
        a[p, :8] = np.random.permutation(np.resize(levels, 8))
        for g in range(8):
            far = levels[np.abs(levels - a[p, g]) >= 10]
            a[p, g + 8] = far[np.random.randint(len(far))]
    return np.exp2(a.ravel()).repeat(32)


def f64(x):
    return np.asarray(x).astype(np.float64)


def striped(idx):
    return np.tile(np.asarray(idx).reshape(-1, 16).T, (8, 1)).astype(np.uint16)


def unstriped(offs):
    return offs[:16].T.reshape(-1).astype(np.int64)


def striped8(idx):
    return np.asarray(idx).reshape(8, -1, 16).transpose(0, 2, 1).reshape(128, -1).astype(np.uint16)


def unstriped8(offs):
    return offs.reshape(8, 16, -1).transpose(0, 2, 1).reshape(8, -1).astype(np.int64)


def pick8(x, idx, run):
    r = np.arange(len(x))
    return x[r[:, None], idx[r % (8 * run) // run]]


E2M1 = np.array([0.0, 0.5, 1.0, 1.5, 2.0, 3.0, 4.0, 6.0, -0.0, -0.5, -1.0, -1.5, -2.0, -3.0, -4.0, -6.0])


def pack_weight(w, fmt):
    k, n = w.shape
    w = f64(np.asarray(w, np.float32).astype(ml_dtypes.bfloat16)).reshape(k // 32, 32, n)
    amax = np.abs(w).max(1)
    if fmt == "e4m3":
        byte = np.frexp(amax)[1] - 1 + 127 - 7
    else:
        mant, ex = np.frexp(amax / 6.0)
        byte = np.where(mant > 0.5, ex, ex - 1) + 127
    byte = np.clip(np.where(amax > 0, byte, 1), 1, 254)
    scaled = (w * np.exp2(127.0 - byte)[:, None, :]).reshape(k, n).astype(np.float32)
    by_word = np.ascontiguousarray(scaled.reshape(k // 512, 128, 4, n).transpose(0, 1, 3, 2))
    if fmt == "e4m3":
        words = by_word.astype(ml_dtypes.float8_e4m3fn).view(np.uint8)
    else:
        c = by_word.astype(ml_dtypes.float4_e2m1fn).view(np.uint8) & 0xF
        words = (c[..., 0::2] | (c[..., 1::2] << 4)).reshape(k // 512, 128, 2 * n)
    return np.ascontiguousarray(words), np.ascontiguousarray(byte.astype(np.uint8).reshape(k // 512, 16, n))


def unpack_weight(words, scales, fmt):
    g, _, n = scales.shape
    words = np.ascontiguousarray(words).reshape(g, 128, n, -1)
    if fmt == "e4m3":
        vals = words.view(ml_dtypes.float8_e4m3fn).astype(np.float64)
    else:
        nib = np.empty((g, 128, n, 4), np.uint8)
        nib[..., 0::2] = words & 0xF
        nib[..., 1::2] = words >> 4
        vals = E2M1[nib]
    vals = vals * np.repeat(np.exp2(scales.astype(np.float64) - 127.0), 8, axis=1)[..., None]
    return vals.transpose(0, 1, 3, 2).reshape(g * 512, n)


def sigmoid(v):
    return 1.0 / (1.0 + np.exp(-v))


K, R, F, T, J, M = 512, 128, 512, 2048, 512, 256


def setup_inputs():
    n = np.random.standard_normal
    idx = np.random.permutation(T)[:J]
    idx2 = np.stack([np.random.permutation(J)[:M] for _ in range(8)])
    idx3 = np.stack([np.random.permutation(J)[:M] for _ in range(8)])
    fk = mx_kscale(K)
    ff = mx_kscale(F)
    tabp = pack_weight(n((K, T)) / fk[:, None], "e2m1")
    return {
        "tab_words": tabp[0],
        "tab_scales": tabp[1],
        "w1": (n((K, R)) * 1 / np.sqrt(K) * fk[:, None]).astype(np.float32),
        "gain": (np.random.uniform(0.5, 1.5, (R, 1))).astype(np.float32),
        "wo": (n((F, R)) * 1 / np.sqrt(F) * ff[:, None]).astype(np.float32),
        "dy": (n((F, M)) / ff[:, None]).astype(np.float32),
        "og": (np.random.uniform(0.3, 1.0, (R, 1))).astype(np.float32),
        "base": (0.3 * n((R, J))).astype(np.float32),
        "offs": striped(idx),
        "offs2": striped8(idx2),
        "offs3": striped8(idx3),
    }


def reference(tab_words, tab_scales, w1, gain, wo, dy, og, base, offs, offs2, offs3):
    idx = unstriped(offs)
    idx2 = unstriped8(offs2)
    idx3 = unstriped8(offs3)
    tabu = unpack_weight(tab_words, tab_scales, "e2m1")
    w1q = mxq(f64(w1), 0, "e4m3")
    tabidxg = tabu[:, idx]
    a = w1q.T @ tabidxg
    h1 = a * f64(gain)
    woq = mxq(f64(wo), 0, "e4m3")
    dyq = mxq(f64(dy), 0, "e4m3")
    c0 = woq.T @ dyq
    e1 = c0 * sigmoid(pick8(h1, idx3, 16))
    s1 = np.zeros((R, J))
    s1[np.arange(R)[:, None], idx2[np.arange(R) % 128 // 16]] = e1
    e2 = c0 * pick8(h1, idx2, 16) * sigmoid(pick8(h1, idx3, 16)) * (1.0 - sigmoid(pick8(h1, idx3, 16)))
    s2 = np.zeros((R, J))
    s2[np.arange(R)[:, None], idx3[np.arange(R) % 128 // 16]] = e2
    e3 = c0 * (-1.0) * sigmoid(pick8(h1, idx3, 16))
    s3 = np.zeros((R, J))
    s3[np.arange(R)[:, None], idx3[np.arange(R) % 128 // 16]] = e3
    dh1 = s1 + s2 + s3
    da = dh1 * f64(gain)
    hda = da * 2.0
    hdh1 = hda * f64(gain)
    he3 = pick8(hdh1, idx3, 16)
    he2 = pick8(hdh1, idx3, 16)
    he1 = pick8(hdh1, idx2, 16)
    e51 = he3 * c0 * (-1.0) * sigmoid(pick8(h1, idx3, 16)) * (1.0 - sigmoid(pick8(h1, idx3, 16)))
    s51 = np.zeros((R, J))
    s51[np.arange(R)[:, None], idx3[np.arange(R) % 128 // 16]] = e51
    e52 = he2 * (1.0 - sigmoid(pick8(h1, idx3, 16))) * c0 * pick8(h1, idx2, 16) * sigmoid(pick8(h1, idx3, 16)) * (1.0 - sigmoid(pick8(h1, idx3, 16)))
    s52 = np.zeros((R, J))
    s52[np.arange(R)[:, None], idx3[np.arange(R) % 128 // 16]] = e52
    e53 = he2 * c0 * pick8(h1, idx2, 16) * sigmoid(pick8(h1, idx3, 16)) * (-1.0) * sigmoid(pick8(h1, idx3, 16)) * (1.0 - sigmoid(pick8(h1, idx3, 16)))
    s53 = np.zeros((R, J))
    s53[np.arange(R)[:, None], idx3[np.arange(R) % 128 // 16]] = e53
    e54 = he1 * c0 * sigmoid(pick8(h1, idx3, 16)) * (1.0 - sigmoid(pick8(h1, idx3, 16)))
    s54 = np.zeros((R, J))
    s54[np.arange(R)[:, None], idx3[np.arange(R) % 128 // 16]] = e54
    e55 = he2 * (1.0 - sigmoid(pick8(h1, idx3, 16))) * sigmoid(pick8(h1, idx3, 16)) * c0
    s55 = np.zeros((R, J))
    s55[np.arange(R)[:, None], idx2[np.arange(R) % 128 // 16]] = e55
    hh1 = s51 + s52 + s53 + s54 + s55
    ha = hh1 * f64(gain)
    y = ha * f64(og) + f64(base)
    return y

@@ -1,0 +1,160 @@
+from contextlib import ExitStack
+
+import concourse.mybir as mybir
+
+K, R, F, T, J, M = 512, 128, 512, 2048, 512, 256
+FLOPS = 2 * K * R * J + 2 * F * R * M
+
+F32 = mybir.dt.float32
+BF16 = mybir.dt.bfloat16
+I32 = mybir.dt.int32
+U32 = mybir.dt.uint32
+U16 = mybir.dt.uint16
+U8 = mybir.dt.uint8
+FP8X4 = mybir.dt.float8_e4m3fn_x4
+FP4X4 = mybir.dt.float4_e2m1fn_x4
+ACT = mybir.ActivationFunctionType
+ALU = mybir.AluOpType
+
+P = 128
+PACK = 4
+HALF = J // 2
+
+
+def tile_attend_gppairgates_kernel(tc, tab_words, tab_scales, w1, gain, wo, dy, og, base, offs, offs2, offs3, out):
+    nc = tc.nc
+    with ExitStack() as ctx:
+        lists = ctx.enter_context(tc.tile_pool(name="lists", bufs=1))
+        sb = ctx.enter_context(tc.tile_pool(name="sb", bufs=1))
+        ps = ctx.enter_context(tc.psum_pool(name="ps", bufs=1))
+
+        def f32(name, width):
+            return sb.tile([P, width], F32, name=name, align_bytes=64)
+
+        slots = lists.tile([P, J // 16], U16, name="slots")
+        picks2 = lists.tile([P, M // 16], U16, name="picks2")
+        picks3 = lists.tile([P, M // 16], U16, name="picks3")
+
+        words = sb.tile([P, T], U16, name="words", align_bytes=64)
+        scales = sb.tile([P, T], U8, name="scales", align_bytes=64)
+        w1_raw = sb.tile([P, PACK, R], F32, name="w1_raw", align_bytes=64)
+        wo_raw = sb.tile([P, PACK, R], F32, name="wo_raw", align_bytes=64)
+        dy_raw = sb.tile([P, PACK, M], F32, name="dy_raw", align_bytes=64)
+        g = f32("g", 1)
+        o = f32("o", 1)
+        base_sb = f32("base_sb", J)
+
+        nc.vector.memset(scales[:].bitcast(I32), 0)
+        nc.sync.dma_start(slots[:], offs)
+        nc.sync.dma_start(out=words[:].bitcast(I32), in_=tab_words[0].bitcast(I32))
+        for q in range(4):
+            nc.sync.dma_start(out=scales[32 * q : 32 * q + 4, :].bitcast(I32), in_=tab_scales[0, 4 * q : 4 * q + 4, :].bitcast(I32))
+        nc.scalar.dma_start(out=g[:], in_=gain)
+        nc.scalar.dma_start(out=o[:], in_=og)
+        nc.sync.dma_start(out=w1_raw[:], in_=w1.rearrange("(p t) r -> p t r", t=PACK))
+        nc.sync.dma_start(picks3[:], offs3)
+        nc.sync.dma_start(out=wo_raw[:], in_=wo.rearrange("(p t) r -> p t r", t=PACK))
+        nc.sync.dma_start(out=dy_raw[:], in_=dy.rearrange("(p t) m -> p t m", t=PACK))
+        nc.sync.dma_start(picks2[:], offs2)
+        nc.sync.dma_start(out=base_sb[:], in_=base)
+
+        windows = [f32("win%d" % n, J) for n in range(4)]
+        for win in windows:
+            nc.vector.memset(win[:], 0.0)
+        s1, s23, s3b, s2b = windows
+
+        def interleave(engine_copy, raw, width, name):
+            grouped = sb.tile([P, width, PACK], BF16, name=name, align_bytes=64)
+            engine_copy(
+                grouped[:].rearrange("p (c i) t -> p c t i", i=4),
+                raw[:].rearrange("p t (c i) -> p c t i", i=4),
+            )
+            return grouped
+
+        def quantise(grouped, width, name):
+            codes = sb.tile([P, width], U32, name=name + "_codes", align_bytes=64)
+            plane = sb.tile([P, width], U8, name=name + "_plane", align_bytes=64)
+            nc.vector.quantize_mx(out=codes[:].bitcast(FP8X4), scales=plane[:], in_=grouped[:].rearrange("p c t -> p (c t)"))
+            return codes, plane
+
+        got_words = sb.tile([P, J], U16, name="got_words", align_bytes=64)
+        nc.vector.tensor_copy(got_words[:], words[:].indirect(slots[:]))
+
+        g2 = f32("g2", 1)
+        g2n = f32("g2n", 1)
+        g2h = f32("g2h", 1)
+        kf = f32("kf", 1)
+        go = f32("go", 1)
+        nc.scalar.activation(g2[:], g[:], ACT.Square)
+        nc.scalar.activation(go[:], o[:], ACT.Copy, scale=g[:])
+        nc.scalar.activation(g2n[:], g2[:], ACT.Copy, scale=-1.0)
+        nc.scalar.activation(g2h[:], g2[:], ACT.Copy, scale=-0.5)
+        nc.scalar.activation(kf[:], go[:], ACT.Copy, scale=-0.25)
+
+        w1_bf = interleave(nc.scalar.copy, w1_raw, R, "w1_bf")
+        wo_bf = interleave(nc.scalar.copy, wo_raw, R, "wo_bf")
+        h1 = f32("h1", J)
+        got_scales = [sb.tile([P, HALF], U8, name="got_scales%d" % h, align_bytes=64) for h in range(2)]
+        nc.vector.tensor_copy(got_scales[0][:], scales[:].indirect(slots[:, 0 : HALF // 16]))
+        w1_codes, w1_plane = quantise(w1_bf, R, "w1")
+        nc.vector.tensor_copy(got_scales[1][:], scales[:].indirect(slots[:, HALF // 16 : J // 16]))
+        for h in range(2):
+            cols = slice(h * HALF, (h + 1) * HALF)
+            a = ps.tile([P, HALF], F32, name="a%d" % h)
+            nc.tensor.matmul_mx(
+                out=a[:], lhsT=w1_codes[:].bitcast(FP8X4), lhsT_scale=w1_plane[:],
+                rhs=got_words[:, cols].bitcast(FP4X4), rhs_scale=got_scales[h][:], start=True, stop=True,
+            )
+            nc.scalar.activation(h1[:, cols], a[:], ACT.Copy, scale=g[:])
+
+        dy_bf = interleave(nc.vector.tensor_copy, dy_raw, M, "dy_bf")
+        wo_codes, wo_plane = quantise(wo_bf, R, "wo")
+        dy_codes, dy_plane = quantise(dy_bf, M, "dy")
+        c = ps.tile([P, M], F32, name="c")
+        nc.tensor.matmul_mx(
+            out=c[:], lhsT=wo_codes[:].bitcast(FP8X4), lhsT_scale=wo_plane[:],
+            rhs=dy_codes[:].bitcast(FP8X4), rhs_scale=dy_plane[:], start=True, stop=True,
+        )
+
+        v = f32("v", M)
+        th = f32("th", M)
+        u = f32("u", M)
+        nc.scalar.activation(v[:], h1[:].indirect(picks3[:]), ACT.Copy)
+        nc.scalar.activation(th[:], v[:], ACT.Tanh, scale=0.5)
+        nc.vector.tensor_copy(u[:], h1[:].indirect(picks2[:]))
+
+        cs = f32("cs", M)
+        w = f32("w", M)
+        th2 = f32("th2", M)
+        t1 = f32("t1", M)
+        nc.vector.scalar_tensor_tensor(cs[:], th[:], 1.0, c[:], ALU.add, ALU.mult)
+        nc.vector.scalar_tensor_tensor(w[:], th[:], 1.0, u[:], ALU.subtract, ALU.mult)
+        nc.scalar.activation(th2[:], th[:], ACT.Square)
+        nc.scalar.activation(t1[:], w[:], ACT.Identity, scale=g2h[:], bias=g2n[:])
+        nc.vector.tensor_copy(s1[:].indirect(picks2[:]), cs[:])
+        nc.vector.tensor_tensor(s23[:].indirect(picks3[:]), cs[:], t1[:], ALU.mult)
+
+        q0 = f32("q0", M)
+        x = f32("x", M)
+        hdh1 = f32("hdh1", J)
+        nc.vector.scalar_tensor_tensor(q0[:], th2[:], 1.0, c[:], ALU.subtract, ALU.mult)
+        nc.vector.scalar_tensor_tensor(hdh1[:], s1[:], g2[:], s23[:], ALU.mult, ALU.add)
+        nc.vector.tensor_tensor(x[:], u[:], th[:], ALU.mult)
+
+        h3 = f32("h3", M)
+        h2 = f32("h2", M)
+        b = f32("b", M)
+        b2 = f32("b2", M)
+        part = f32("part", J)
+        res = f32("res", J)
+        nc.vector.tensor_copy(h3[:], hdh1[:].indirect(picks3[:]))
+        nc.scalar.activation(h2[:], hdh1[:].indirect(picks2[:]), ACT.Copy)
+        nc.vector.scalar_tensor_tensor(b[:], x[:], 1.0, h3[:], ALU.add, ALU.mult)
+        nc.vector.tensor_tensor(s2b[:].indirect(picks2[:]), h3[:], q0[:], ALU.mult)
+        nc.vector.tensor_tensor(b2[:], h2[:], b[:], ALU.subtract)
+        nc.vector.scalar_tensor_tensor(part[:], s2b[:], kf[:], base_sb[:], ALU.mult, ALU.add)
+        nc.vector.tensor_tensor(s3b[:].indirect(picks3[:]), b2[:], q0[:], ALU.mult)
+        for h in range(2):
+            cols = slice(h * HALF, (h + 1) * HALF)
+            nc.vector.scalar_tensor_tensor(res[:, cols], s3b[:, cols], kf[:], part[:, cols], ALU.mult, ALU.add)
+            nc.sync.dma_start(out=out[:, cols], in_=res[:, cols])

@@ -1,6 +1,7 @@
 from contextlib import ExitStack
 
 import concourse.mybir as mybir
+from concourse.masks import make_identity
 
 K, R, F, T, J, M = 512, 128, 512, 2048, 512, 256
 FLOPS = 2 * K * R * J + 2 * F * R * M
@@ -19,6 +20,7 @@ ALU = mybir.AluOpType
 P = 128
 PACK = 4
 HALF = J // 2
+MH = M // 2
 
 
 def tile_attend_gppairgates_kernel(tc, tab_words, tab_scales, w1, gain, wo, dy, og, base, offs, offs2, offs3, out):
@@ -28,8 +30,8 @@ def tile_attend_gppairgates_kernel(tc, tab_words, tab_scales, w1, gain, wo, dy, 
         sb = ctx.enter_context(tc.tile_pool(name="sb", bufs=1))
         ps = ctx.enter_context(tc.psum_pool(name="ps", bufs=1))
 
-        def f32(name, width):
-            return sb.tile([P, width], F32, name=name, align_bytes=64)
+        def f32(name, width, tag=None):
+            return sb.tile([P, width], F32, name=name, tag=tag or name, align_bytes=64)
 
         slots = lists.tile([P, J // 16], U16, name="slots")
         picks2 = lists.tile([P, M // 16], U16, name="picks2")
@@ -37,34 +39,33 @@ def tile_attend_gppairgates_kernel(tc, tab_words, tab_scales, w1, gain, wo, dy, 
 
         words = sb.tile([P, T], U16, name="words", align_bytes=64)
         scales = sb.tile([P, T], U8, name="scales", align_bytes=64)
-        w1_raw = sb.tile([P, PACK, R], F32, name="w1_raw", align_bytes=64)
+        w1_raw = sb.tile([P, PACK, R], F32, name="w1_raw", tag="w1_then_scales", align_bytes=64)
         wo_raw = sb.tile([P, PACK, R], F32, name="wo_raw", align_bytes=64)
-        dy_raw = sb.tile([P, PACK, M], F32, name="dy_raw", align_bytes=64)
+        dy_raw = sb.tile([P, PACK, M], F32, name="dy_raw", tag="dy_then_base", align_bytes=64)
         g = f32("g", 1)
         o = f32("o", 1)
-        base_sb = f32("base_sb", J)
 
-        nc.vector.memset(scales[:].bitcast(I32), 0)
+        nc.vector.memset(scales[:, 0 : T // 2].bitcast(I32), 0)
+        nc.gpsimd.memset(scales[:, T // 2 : T].bitcast(I32), 0)
         nc.sync.dma_start(slots[:], offs)
         nc.sync.dma_start(out=words[:].bitcast(I32), in_=tab_words[0].bitcast(I32))
         for q in range(4):
             nc.sync.dma_start(out=scales[32 * q : 32 * q + 4, :].bitcast(I32), in_=tab_scales[0, 4 * q : 4 * q + 4, :].bitcast(I32))
-        nc.scalar.dma_start(out=g[:], in_=gain)
-        nc.scalar.dma_start(out=o[:], in_=og)
         nc.sync.dma_start(out=w1_raw[:], in_=w1.rearrange("(p t) r -> p t r", t=PACK))
-        nc.sync.dma_start(picks3[:], offs3)
         nc.sync.dma_start(out=wo_raw[:], in_=wo.rearrange("(p t) r -> p t r", t=PACK))
         nc.sync.dma_start(out=dy_raw[:], in_=dy.rearrange("(p t) m -> p t m", t=PACK))
+        nc.sync.dma_start(picks3[:], offs3)
         nc.sync.dma_start(picks2[:], offs2)
-        nc.sync.dma_start(out=base_sb[:], in_=base)
+        nc.gpsimd.dma_start(out=g[:], in_=gain)
+        nc.gpsimd.dma_start(out=o[:], in_=og)
 
         windows = [f32("win%d" % n, J) for n in range(4)]
         for win in windows:
             nc.vector.memset(win[:], 0.0)
         s1, s23, s3b, s2b = windows
 
-        def interleave(engine_copy, raw, width, name):
-            grouped = sb.tile([P, width, PACK], BF16, name=name, align_bytes=64)
+        def interleave(engine_copy, raw, width, name, tag):
+            grouped = sb.tile([P, width, PACK], BF16, name=name, tag=tag, align_bytes=64)
             engine_copy(
                 grouped[:].rearrange("p (c i) t -> p c t i", i=4),
                 raw[:].rearrange("p t (c i) -> p c t i", i=4),
@@ -77,38 +78,47 @@ def tile_attend_gppairgates_kernel(tc, tab_words, tab_scales, w1, gain, wo, dy, 
             nc.vector.quantize_mx(out=codes[:].bitcast(FP8X4), scales=plane[:], in_=grouped[:].rearrange("p c t -> p (c t)"))
             return codes, plane
 
-        got_words = sb.tile([P, J], U16, name="got_words", align_bytes=64)
-        nc.vector.tensor_copy(got_words[:], words[:].indirect(slots[:]))
-
         g2 = f32("g2", 1)
         g2n = f32("g2n", 1)
         g2h = f32("g2h", 1)
         kf = f32("kf", 1)
-        go = f32("go", 1)
-        nc.scalar.activation(g2[:], g[:], ACT.Square)
-        nc.scalar.activation(go[:], o[:], ACT.Copy, scale=g[:])
-        nc.scalar.activation(g2n[:], g2[:], ACT.Copy, scale=-1.0)
-        nc.scalar.activation(g2h[:], g2[:], ACT.Copy, scale=-0.5)
-        nc.scalar.activation(kf[:], go[:], ACT.Copy, scale=-0.25)
+        kfn = f32("kfn", 1)
+        nc.gpsimd.tensor_tensor(g2[:], g[:], g[:], ALU.mult)
+        nc.gpsimd.tensor_scalar(g2n[:], g2[:], -1.0, 0.0, ALU.mult, ALU.add)
+        nc.gpsimd.tensor_scalar(g2h[:], g2[:], -0.5, 0.0, ALU.mult, ALU.add)
+        nc.gpsimd.tensor_scalar(kf[:], o[:], g[:], -0.25, ALU.mult, ALU.mult)
+        nc.gpsimd.tensor_scalar(kfn[:], o[:], g[:], 0.25, ALU.mult, ALU.mult)
 
-        w1_bf = interleave(nc.scalar.copy, w1_raw, R, "w1_bf")
-        wo_bf = interleave(nc.scalar.copy, wo_raw, R, "wo_bf")
-        h1 = f32("h1", J)
-        got_scales = [sb.tile([P, HALF], U8, name="got_scales%d" % h, align_bytes=64) for h in range(2)]
+        ident = f32("ident", P)
+        make_identity(nc, ident[:])
+
+        got_words = sb.tile([P, J], U16, name="got_words", align_bytes=64)
+        nc.vector.tensor_copy(got_words[:], words[:].indirect(slots[:]))
+        w1_bf = interleave(nc.scalar.copy, w1_raw, R, "w1_bf", "w1_bf")
+        wo_bf = interleave(nc.scalar.copy, wo_raw, R, "wo_bf", "wo_bf_then_dy_bf")
+
+        got_scales = [
+            sb.tile([P, HALF], U8, name="got_scales0", align_bytes=64),
+            sb.tile([P, HALF], U8, name="got_scales1", tag="w1_then_scales", align_bytes=64),
+        ]
         nc.vector.tensor_copy(got_scales[0][:], scales[:].indirect(slots[:, 0 : HALF // 16]))
         w1_codes, w1_plane = quantise(w1_bf, R, "w1")
         nc.vector.tensor_copy(got_scales[1][:], scales[:].indirect(slots[:, HALF // 16 : J // 16]))
+
+        h1 = f32("h1", J)
         for h in range(2):
             cols = slice(h * HALF, (h + 1) * HALF)
-            a = ps.tile([P, HALF], F32, name="a%d" % h)
+            a = ps.tile([P, HALF], F32, name="a%d" % h, tag="half%d" % h)
             nc.tensor.matmul_mx(
                 out=a[:], lhsT=w1_codes[:].bitcast(FP8X4), lhsT_scale=w1_plane[:],
                 rhs=got_words[:, cols].bitcast(FP4X4), rhs_scale=got_scales[h][:], start=True, stop=True,
             )
             nc.scalar.activation(h1[:, cols], a[:], ACT.Copy, scale=g[:])
 
-        dy_bf = interleave(nc.vector.tensor_copy, dy_raw, M, "dy_bf")
         wo_codes, wo_plane = quantise(wo_bf, R, "wo")
+        dy_bf = interleave(nc.vector.tensor_copy, dy_raw, M, "dy_bf", "wo_bf_then_dy_bf")
+        base_sb = f32("base_sb", J, "dy_then_base")
+        nc.sync.dma_start(out=base_sb[:], in_=base)
         dy_codes, dy_plane = quantise(dy_bf, M, "dy")
         c = ps.tile([P, M], F32, name="c")
         nc.tensor.matmul_mx(
@@ -119,25 +129,28 @@ def tile_attend_gppairgates_kernel(tc, tab_words, tab_scales, w1, gain, wo, dy, 
         v = f32("v", M)
         th = f32("th", M)
         u = f32("u", M)
-        nc.scalar.activation(v[:], h1[:].indirect(picks3[:]), ACT.Copy)
+        nc.scalar.activation(v[:, 0:MH], h1[:].indirect(picks3[:, 0 : MH // 16]), ACT.Copy)
+        nc.vector.tensor_copy(v[:, MH:M], h1[:].indirect(picks3[:, MH // 16 : M // 16]))
         nc.scalar.activation(th[:], v[:], ACT.Tanh, scale=0.5)
         nc.vector.tensor_copy(u[:], h1[:].indirect(picks2[:]))
 
-        cs = f32("cs", M)
+        cs = f32("cs", M, "cs_then_q")
         w = f32("w", M)
         th2 = f32("th2", M)
-        t1 = f32("t1", M)
+        mk = f32("mk", M)
+        t1 = f32("t1", M, "t1_then_x")
         nc.vector.scalar_tensor_tensor(cs[:], th[:], 1.0, c[:], ALU.add, ALU.mult)
         nc.vector.scalar_tensor_tensor(w[:], th[:], 1.0, u[:], ALU.subtract, ALU.mult)
-        nc.scalar.activation(th2[:], th[:], ACT.Square)
         nc.scalar.activation(t1[:], w[:], ACT.Identity, scale=g2h[:], bias=g2n[:])
+        nc.scalar.activation(th2[:], th[:], ACT.Square)
+        nc.scalar.activation(mk[:], th2[:], ACT.Identity, scale=kf[:], bias=kfn[:])
         nc.vector.tensor_copy(s1[:].indirect(picks2[:]), cs[:])
         nc.vector.tensor_tensor(s23[:].indirect(picks3[:]), cs[:], t1[:], ALU.mult)
 
-        q0 = f32("q0", M)
-        x = f32("x", M)
+        q = f32("q", M, "cs_then_q")
+        x = f32("x", M, "t1_then_x")
         hdh1 = f32("hdh1", J)
-        nc.vector.scalar_tensor_tensor(q0[:], th2[:], 1.0, c[:], ALU.subtract, ALU.mult)
+        nc.vector.tensor_tensor(q[:], c[:], mk[:], ALU.mult)
         nc.vector.scalar_tensor_tensor(hdh1[:], s1[:], g2[:], s23[:], ALU.mult, ALU.add)
         nc.vector.tensor_tensor(x[:], u[:], th[:], ALU.mult)
 
@@ -145,16 +158,30 @@ def tile_attend_gppairgates_kernel(tc, tab_words, tab_scales, w1, gain, wo, dy, 
         h2 = f32("h2", M)
         b = f32("b", M)
         b2 = f32("b2", M)
-        part = f32("part", J)
-        res = f32("res", J)
-        nc.vector.tensor_copy(h3[:], hdh1[:].indirect(picks3[:]))
         nc.scalar.activation(h2[:], hdh1[:].indirect(picks2[:]), ACT.Copy)
-        nc.vector.scalar_tensor_tensor(b[:], x[:], 1.0, h3[:], ALU.add, ALU.mult)
-        nc.vector.tensor_tensor(s2b[:].indirect(picks2[:]), h3[:], q0[:], ALU.mult)
-        nc.vector.tensor_tensor(b2[:], h2[:], b[:], ALU.subtract)
-        nc.vector.scalar_tensor_tensor(part[:], s2b[:], kf[:], base_sb[:], ALU.mult, ALU.add)
-        nc.vector.tensor_tensor(s3b[:].indirect(picks3[:]), b2[:], q0[:], ALU.mult)
+        halves = [slice(h * MH, (h + 1) * MH) for h in range(2)]
         for h in range(2):
-            cols = slice(h * HALF, (h + 1) * HALF)
-            nc.vector.scalar_tensor_tensor(res[:, cols], s3b[:, cols], kf[:], part[:, cols], ALU.mult, ALU.add)
+            nc.vector.tensor_copy(h3[:, halves[h]], hdh1[:].indirect(picks3[:, h * MH // 16 : (h + 1) * MH // 16]))
+        for cols in halves:
+            nc.vector.scalar_tensor_tensor(b[:, cols], x[:, cols], 1.0, h3[:, cols], ALU.add, ALU.mult)
+        for cols in halves:
+            nc.vector.tensor_tensor(b2[:, cols], h2[:, cols], b[:, cols], ALU.subtract)
+        nc.vector.tensor_tensor(s2b[:].indirect(picks2[:]), h3[:], q[:], ALU.mult)
+        nc.vector.tensor_tensor(s3b[:].indirect(picks3[:]), b2[:], q[:], ALU.mult)
+
+        blocks = [slice(n * P, (n + 1) * P) for n in range(J // P)]
+        turned = [ps.tile([P, P], F32, name="turned%d" % n) for n in range(J // P)]
+        for n, cols in enumerate(blocks):
+            nc.tensor.matmul(turned[n][:], base_sb[:, cols], ident[:], start=True, stop=False, is_transpose=True)
+        part_t = f32("part_t", J)
+        for n, cols in enumerate(blocks):
+            nc.tensor.matmul(turned[n][:], s2b[:, cols], ident[:], start=False, stop=True, is_transpose=True)
+            nc.scalar.copy(part_t[:, cols], turned[n][:])
+        res = f32("res", J)
+        for h, group in enumerate((blocks[:2], blocks[2:])):
+            cols = slice(group[0].start, group[-1].stop)
+            part = ps.tile([P, len(group) * P], F32, name="part%d" % h, tag="half%d" % h)
+            for n, block in enumerate(group):
+                nc.tensor.transpose(part[:, n * P : (n + 1) * P], part_t[:, block], ident[:])
+            nc.vector.tensor_tensor(res[:, cols], part[:], s3b[:, cols], ALU.add)
             nc.sync.dma_start(out=out[:, cols], in_=res[:, cols])

@@ -59,6 +59,11 @@ def tile_attend_gppairgates_kernel(tc, tab_words, tab_scales, w1, gain, wo, dy, 
         nc.gpsimd.dma_start(out=g[:], in_=gain)
         nc.gpsimd.dma_start(out=o[:], in_=og)
 
+        warm_in = f32("warm_in", 1)
+        warm_out = f32("warm_out", 1)
+        nc.vector.memset(warm_in[:], 0.0)
+        nc.scalar.activation(warm_out[:], warm_in[:], ACT.Sigmoid)
+
         windows = [f32("win%d" % n, J) for n in range(4)]
         for win in windows:
             nc.vector.memset(win[:], 0.0)
@@ -78,14 +83,10 @@ def tile_attend_gppairgates_kernel(tc, tab_words, tab_scales, w1, gain, wo, dy, 
             nc.vector.quantize_mx(out=codes[:].bitcast(FP8X4), scales=plane[:], in_=grouped[:].rearrange("p c t -> p (c t)"))
             return codes, plane
 
-        g2 = f32("g2", 1)
-        g2n = f32("g2n", 1)
-        g2h = f32("g2h", 1)
+        k2 = f32("k2", 1)
         kf = f32("kf", 1)
         kfn = f32("kfn", 1)
-        nc.gpsimd.tensor_tensor(g2[:], g[:], g[:], ALU.mult)
-        nc.gpsimd.tensor_scalar(g2n[:], g2[:], -1.0, 0.0, ALU.mult, ALU.add)
-        nc.gpsimd.tensor_scalar(g2h[:], g2[:], -0.5, 0.0, ALU.mult, ALU.add)
+        nc.gpsimd.tensor_scalar(k2[:], g[:], g[:], 2.0, ALU.mult, ALU.mult)
         nc.gpsimd.tensor_scalar(kf[:], o[:], g[:], -0.25, ALU.mult, ALU.mult)
         nc.gpsimd.tensor_scalar(kfn[:], o[:], g[:], 0.25, ALU.mult, ALU.mult)
 
@@ -126,12 +127,10 @@ def tile_attend_gppairgates_kernel(tc, tab_words, tab_scales, w1, gain, wo, dy, 
             rhs=dy_codes[:].bitcast(FP8X4), rhs_scale=dy_plane[:], start=True, stop=True,
         )
 
-        v = f32("v", M)
+        s = f32("s", M)
         th = f32("th", M)
         u = f32("u", M)
-        nc.scalar.activation(v[:, 0:MH], h1[:].indirect(picks3[:, 0 : MH // 16]), ACT.Copy)
-        nc.vector.tensor_copy(v[:, MH:M], h1[:].indirect(picks3[:, MH // 16 : M // 16]))
-        nc.scalar.activation(th[:], v[:], ACT.Tanh, scale=0.5)
+        nc.scalar.activation(s[:], h1[:].indirect(picks3[:]), ACT.Sigmoid)
         nc.vector.tensor_copy(u[:], h1[:].indirect(picks2[:]))
 
         cs = f32("cs", M, "cs_then_q")
@@ -139,9 +138,10 @@ def tile_attend_gppairgates_kernel(tc, tab_words, tab_scales, w1, gain, wo, dy, 
         th2 = f32("th2", M)
         mk = f32("mk", M)
         t1 = f32("t1", M, "t1_then_x")
-        nc.vector.scalar_tensor_tensor(cs[:], th[:], 1.0, c[:], ALU.add, ALU.mult)
-        nc.vector.scalar_tensor_tensor(w[:], th[:], 1.0, u[:], ALU.subtract, ALU.mult)
-        nc.scalar.activation(t1[:], w[:], ACT.Identity, scale=g2h[:], bias=g2n[:])
+        nc.vector.scalar_tensor_tensor(cs[:], c[:], k2[:], s[:], ALU.mult, ALU.mult)
+        nc.vector.scalar_tensor_tensor(w[:], s[:], 1.0, u[:], ALU.subtract, ALU.mult)
+        nc.scalar.activation(t1[:], w[:], ACT.Copy, scale=-1.0, bias=-1.0)
+        nc.scalar.activation(th[:], s[:], ACT.Copy, scale=2.0, bias=-1.0)
         nc.scalar.activation(th2[:], th[:], ACT.Square)
         nc.scalar.activation(mk[:], th2[:], ACT.Identity, scale=kf[:], bias=kfn[:])
         nc.vector.tensor_copy(s1[:].indirect(picks2[:]), cs[:])
@@ -151,7 +151,7 @@ def tile_attend_gppairgates_kernel(tc, tab_words, tab_scales, w1, gain, wo, dy, 
         x = f32("x", M, "t1_then_x")
         hdh1 = f32("hdh1", J)
         nc.vector.tensor_tensor(q[:], c[:], mk[:], ALU.mult)
-        nc.vector.scalar_tensor_tensor(hdh1[:], s1[:], g2[:], s23[:], ALU.mult, ALU.add)
+        nc.vector.tensor_tensor(hdh1[:], s1[:], s23[:], ALU.add)
         nc.vector.tensor_tensor(x[:], u[:], th[:], ALU.mult)
 
         h3 = f32("h3", M)

from contextlib import ExitStack

import concourse.mybir as mybir
from concourse.masks import make_identity

K, R, F, T, J, M = 512, 128, 512, 2048, 512, 256
FLOPS = 2 * K * R * J + 2 * F * R * M

F32 = mybir.dt.float32
BF16 = mybir.dt.bfloat16
I32 = mybir.dt.int32
U32 = mybir.dt.uint32
U16 = mybir.dt.uint16
U8 = mybir.dt.uint8
FP8X4 = mybir.dt.float8_e4m3fn_x4
FP4X4 = mybir.dt.float4_e2m1fn_x4
ACT = mybir.ActivationFunctionType
ALU = mybir.AluOpType

P = 128
PACK = 4
HALF = J // 2
MH = M // 2


def tile_attend_gppairgates_kernel(tc, tab_words, tab_scales, w1, gain, wo, dy, og, base, offs, offs2, offs3, out):
    nc = tc.nc
    with ExitStack() as ctx:
        lists = ctx.enter_context(tc.tile_pool(name="lists", bufs=1))
        sb = ctx.enter_context(tc.tile_pool(name="sb", bufs=1))
        ps = ctx.enter_context(tc.psum_pool(name="ps", bufs=1))

        def f32(name, width, tag=None):
            return sb.tile([P, width], F32, name=name, tag=tag or name, align_bytes=64)

        slots = lists.tile([P, J // 16], U16, name="slots")
        picks2 = lists.tile([P, M // 16], U16, name="picks2")
        picks3 = lists.tile([P, M // 16], U16, name="picks3")

        words = sb.tile([P, T], U16, name="words", align_bytes=64)
        scales = sb.tile([P, T], U8, name="scales", align_bytes=64)
        w1_raw = sb.tile([P, PACK, R], F32, name="w1_raw", tag="w1_then_scales", align_bytes=64)
        wo_raw = sb.tile([P, PACK, R], F32, name="wo_raw", align_bytes=64)
        dy_raw = sb.tile([P, PACK, M], F32, name="dy_raw", tag="dy_then_base", align_bytes=64)
        g = f32("g", 1)
        o = f32("o", 1)

        nc.vector.memset(scales[:, 0 : T // 2].bitcast(I32), 0)
        nc.gpsimd.memset(scales[:, T // 2 : T].bitcast(I32), 0)
        nc.sync.dma_start(slots[:], offs)
        nc.sync.dma_start(out=words[:].bitcast(I32), in_=tab_words[0].bitcast(I32))
        for q in range(4):
            nc.sync.dma_start(out=scales[32 * q : 32 * q + 4, :].bitcast(I32), in_=tab_scales[0, 4 * q : 4 * q + 4, :].bitcast(I32))
        nc.sync.dma_start(out=w1_raw[:], in_=w1.rearrange("(p t) r -> p t r", t=PACK))
        nc.sync.dma_start(out=wo_raw[:], in_=wo.rearrange("(p t) r -> p t r", t=PACK))
        nc.sync.dma_start(out=dy_raw[:], in_=dy.rearrange("(p t) m -> p t m", t=PACK))
        nc.sync.dma_start(picks3[:], offs3)
        nc.sync.dma_start(picks2[:], offs2)
        nc.gpsimd.dma_start(out=g[:], in_=gain)
        nc.gpsimd.dma_start(out=o[:], in_=og)

        warm_in = f32("warm_in", 1)
        warm_out = f32("warm_out", 1)
        nc.vector.memset(warm_in[:], 0.0)
        nc.scalar.activation(warm_out[:], warm_in[:], ACT.Sigmoid)

        windows = [f32("win%d" % n, J) for n in range(4)]
        for win in windows:
            nc.vector.memset(win[:], 0.0)
        s1, s23, s3b, s2b = windows

        def interleave(engine_copy, raw, width, name, tag):
            grouped = sb.tile([P, width, PACK], BF16, name=name, tag=tag, align_bytes=64)
            engine_copy(
                grouped[:].rearrange("p (c i) t -> p c t i", i=4),
                raw[:].rearrange("p t (c i) -> p c t i", i=4),
            )
            return grouped

        def quantise(grouped, width, name):
            codes = sb.tile([P, width], U32, name=name + "_codes", align_bytes=64)
            plane = sb.tile([P, width], U8, name=name + "_plane", align_bytes=64)
            nc.vector.quantize_mx(out=codes[:].bitcast(FP8X4), scales=plane[:], in_=grouped[:].rearrange("p c t -> p (c t)"))
            return codes, plane

        k2 = f32("k2", 1)
        kf = f32("kf", 1)
        kfn = f32("kfn", 1)
        nc.gpsimd.tensor_scalar(k2[:], g[:], g[:], 2.0, ALU.mult, ALU.mult)
        nc.gpsimd.tensor_scalar(kf[:], o[:], g[:], -0.25, ALU.mult, ALU.mult)
        nc.gpsimd.tensor_scalar(kfn[:], o[:], g[:], 0.25, ALU.mult, ALU.mult)

        ident = f32("ident", P)
        make_identity(nc, ident[:])

        got_words = sb.tile([P, J], U16, name="got_words", align_bytes=64)
        nc.vector.tensor_copy(got_words[:], words[:].indirect(slots[:]))
        w1_bf = interleave(nc.scalar.copy, w1_raw, R, "w1_bf", "w1_bf")
        wo_bf = interleave(nc.scalar.copy, wo_raw, R, "wo_bf", "wo_bf_then_dy_bf")

        got_scales = [
            sb.tile([P, HALF], U8, name="got_scales0", align_bytes=64),
            sb.tile([P, HALF], U8, name="got_scales1", tag="w1_then_scales", align_bytes=64),
        ]
        nc.vector.tensor_copy(got_scales[0][:], scales[:].indirect(slots[:, 0 : HALF // 16]))
        w1_codes, w1_plane = quantise(w1_bf, R, "w1")
        nc.vector.tensor_copy(got_scales[1][:], scales[:].indirect(slots[:, HALF // 16 : J // 16]))

        h1 = f32("h1", J)
        for h in range(2):
            cols = slice(h * HALF, (h + 1) * HALF)
            a = ps.tile([P, HALF], F32, name="a%d" % h, tag="half%d" % h)
            nc.tensor.matmul_mx(
                out=a[:], lhsT=w1_codes[:].bitcast(FP8X4), lhsT_scale=w1_plane[:],
                rhs=got_words[:, cols].bitcast(FP4X4), rhs_scale=got_scales[h][:], start=True, stop=True,
            )
            nc.scalar.activation(h1[:, cols], a[:], ACT.Copy, scale=g[:])

        wo_codes, wo_plane = quantise(wo_bf, R, "wo")
        dy_bf = interleave(nc.vector.tensor_copy, dy_raw, M, "dy_bf", "wo_bf_then_dy_bf")
        base_sb = f32("base_sb", J, "dy_then_base")
        nc.sync.dma_start(out=base_sb[:], in_=base)
        dy_codes, dy_plane = quantise(dy_bf, M, "dy")
        c = ps.tile([P, M], F32, name="c")
        nc.tensor.matmul_mx(
            out=c[:], lhsT=wo_codes[:].bitcast(FP8X4), lhsT_scale=wo_plane[:],
            rhs=dy_codes[:].bitcast(FP8X4), rhs_scale=dy_plane[:], start=True, stop=True,
        )

        s = f32("s", M)
        th = f32("th", M)
        u = f32("u", M)
        nc.scalar.activation(s[:], h1[:].indirect(picks3[:]), ACT.Sigmoid)
        nc.vector.tensor_copy(u[:], h1[:].indirect(picks2[:]))

        cs = f32("cs", M, "cs_then_q")
        w = f32("w", M)
        th2 = f32("th2", M)
        mk = f32("mk", M)
        t1 = f32("t1", M, "t1_then_x")
        nc.vector.scalar_tensor_tensor(cs[:], c[:], k2[:], s[:], ALU.mult, ALU.mult)
        nc.vector.scalar_tensor_tensor(w[:], s[:], 1.0, u[:], ALU.subtract, ALU.mult)
        nc.scalar.activation(t1[:], w[:], ACT.Copy, scale=-1.0, bias=-1.0)
        nc.scalar.activation(th[:], s[:], ACT.Copy, scale=2.0, bias=-1.0)
        nc.scalar.activation(th2[:], th[:], ACT.Square)
        nc.scalar.activation(mk[:], th2[:], ACT.Identity, scale=kf[:], bias=kfn[:])
        nc.vector.tensor_copy(s1[:].indirect(picks2[:]), cs[:])
        nc.vector.tensor_tensor(s23[:].indirect(picks3[:]), cs[:], t1[:], ALU.mult)

        q = f32("q", M, "cs_then_q")
        x = f32("x", M, "t1_then_x")
        hdh1 = f32("hdh1", J)
        nc.vector.tensor_tensor(q[:], c[:], mk[:], ALU.mult)
        nc.vector.tensor_tensor(hdh1[:], s1[:], s23[:], ALU.add)
        nc.vector.tensor_tensor(x[:], u[:], th[:], ALU.mult)

        h3 = f32("h3", M)
        h2 = f32("h2", M)
        b = f32("b", M)
        b2 = f32("b2", M)
        nc.scalar.activation(h2[:], hdh1[:].indirect(picks2[:]), ACT.Copy)
        halves = [slice(h * MH, (h + 1) * MH) for h in range(2)]
        for h in range(2):
            nc.vector.tensor_copy(h3[:, halves[h]], hdh1[:].indirect(picks3[:, h * MH // 16 : (h + 1) * MH // 16]))
        for cols in halves:
            nc.vector.scalar_tensor_tensor(b[:, cols], x[:, cols], 1.0, h3[:, cols], ALU.add, ALU.mult)
        for cols in halves:
            nc.vector.tensor_tensor(b2[:, cols], h2[:, cols], b[:, cols], ALU.subtract)
        nc.vector.tensor_tensor(s2b[:].indirect(picks2[:]), h3[:], q[:], ALU.mult)
        nc.vector.tensor_tensor(s3b[:].indirect(picks3[:]), b2[:], q[:], ALU.mult)

        blocks = [slice(n * P, (n + 1) * P) for n in range(J // P)]
        turned = [ps.tile([P, P], F32, name="turned%d" % n) for n in range(J // P)]
        for n, cols in enumerate(blocks):
            nc.tensor.matmul(turned[n][:], base_sb[:, cols], ident[:], start=True, stop=False, is_transpose=True)
        part_t = f32("part_t", J)
        for n, cols in enumerate(blocks):
            nc.tensor.matmul(turned[n][:], s2b[:, cols], ident[:], start=False, stop=True, is_transpose=True)
            nc.scalar.copy(part_t[:, cols], turned[n][:])
        res = f32("res", J)
        for h, group in enumerate((blocks[:2], blocks[2:])):
            cols = slice(group[0].start, group[-1].stop)
            part = ps.tile([P, len(group) * P], F32, name="part%d" % h, tag="half%d" % h)
            for n, block in enumerate(group):
                nc.tensor.transpose(part[:, n * P : (n + 1) * P], part_t[:, block], ident[:])
            nc.vector.tensor_tensor(res[:, cols], part[:], s3b[:, cols], ALU.add)
            nc.sync.dma_start(out=out[:, cols], in_=res[:, cols])
